import numpy as np
import ml_dtypes


def mxq(x, axis, fmt="e4m3"):
    dtype, down = {"e4m3": (ml_dtypes.float8_e4m3fn, 7), "e5m2": (ml_dtypes.float8_e5m2, 14)}[fmt]
    v = np.moveaxis(np.asarray(x, np.float32).astype(ml_dtypes.bfloat16).astype(np.float64), axis, -1)
    blocks = v.reshape(v.shape[:-1] + (-1, 32))
    amax = np.abs(blocks).max(-1, keepdims=True)
    byte = np.maximum(np.where(amax > 0, np.frexp(amax)[1] - 1 + 127, 0) - down, 1)
    scale = np.exp2(byte - 127.0)
    codes = (blocks / scale).astype(np.float32).astype(dtype).astype(np.float64)
    return np.moveaxis((codes * scale).reshape(v.shape), -1, axis)


WIDE = False


def mx_kscale(k):
    if not WIDE:
        return np.ones(k)
    levels = np.array([10, -10, 5, -5, 0])
    if k % 512:
        return np.exp2(np.random.permutation(np.resize(levels, k // 32))).repeat(32)
    a = np.empty((k // 512, 16))
    for p in range(k // 512):
        a[p, :8] = np.random.permutation(np.resize(levels, 8))
        for g in range(8):
            far = levels[np.abs(levels - a[p, g]) >= 10]
            a[p, g + 8] = far[np.random.randint(len(far))]
    return np.exp2(a.ravel()).repeat(32)


BF16 = ml_dtypes.bfloat16


def bf(x):
    return np.asarray(x, np.float32).astype(BF16)


def f64(x):
    return np.asarray(x).astype(np.float64)


E2M1 = np.array([0.0, 0.5, 1.0, 1.5, 2.0, 3.0, 4.0, 6.0, -0.0, -0.5, -1.0, -1.5, -2.0, -3.0, -4.0, -6.0])


def pack_weight(w, fmt):
    k, n = w.shape
    w = f64(bf(w)).reshape(k // 32, 32, n)
    amax = np.abs(w).max(1)
    if fmt == "e4m3":
        byte = np.frexp(amax)[1] - 1 + 127 - 7
    else:
        mant, ex = np.frexp(amax / 6.0)
        byte = np.where(mant > 0.5, ex, ex - 1) + 127
    byte = np.clip(np.where(amax > 0, byte, 1), 1, 254)
    scaled = (w * np.exp2(127.0 - byte)[:, None, :]).reshape(k, n).astype(np.float32)
    by_word = np.ascontiguousarray(scaled.reshape(k // 512, 128, 4, n).transpose(0, 1, 3, 2))
    if fmt == "e4m3":
        words = by_word.astype(ml_dtypes.float8_e4m3fn).view(np.uint8)
    else:
        c = by_word.astype(ml_dtypes.float4_e2m1fn).view(np.uint8) & 0xF
        words = c[..., 0::2] | (c[..., 1::2] << 4)
    return np.ascontiguousarray(words), np.ascontiguousarray(byte.astype(np.uint8).reshape(k // 512, 16, n))


def unpack_weight(words, scales, fmt):
    g, p, n, _ = words.shape
    if fmt == "e4m3":
        vals = np.ascontiguousarray(words).view(ml_dtypes.float8_e4m3fn).astype(np.float64)
    else:
        nib = np.empty((g, p, n, 4), np.uint8)
        nib[..., 0::2] = words & 0xF
        nib[..., 1::2] = words >> 4
        vals = E2M1[nib]
    vals = vals * np.repeat(np.exp2(scales.astype(np.float64) - 127.0), 8, axis=1)[..., None]
    return vals.transpose(0, 1, 3, 2).reshape(g * 512, n)
def pack4(w):
    words, scales = pack_weight(w, "e2m1")
    return words.reshape(words.shape[0], 128, -1), scales


def unpack4(words, scales):
    return unpack_weight(words.reshape(words.shape[0], 128, -1, 2), scales, "e2m1")


M, K, N = 2048, 1024, 1024

FLOOR = 0.25


def setup_inputs():
    s = mx_kscale(K)
    patches = np.random.standard_normal((M, K)) * s
    d_row = np.random.standard_normal((K, N)) / np.sqrt(K) / s[:, None]
    d_col = np.random.standard_normal((K, N)) / np.sqrt(K) / s[:, None]
    d_col_words, d_col_scales = pack4(d_col)
    return {"patches": bf(patches),
            "d_row": bf(d_row),
            "d_col_words": d_col_words,
            "d_col_scales": d_col_scales}


def reference(patches, d_row, d_col_words, d_col_scales):
    x = mxq(f64(patches), 1, "e4m3")
    wr = mxq(f64(d_row), 0, "e4m3")
    wc = unpack4(d_col_words, d_col_scales)
    gr = x @ wr
    gc = x @ wc
    diagonal = gr + gc
    magnitude = np.sqrt(gr * gr + gc * gc + FLOOR * FLOOR)
    return magnitude, diagonal

@@ -1,0 +1,294 @@
+from contextlib import ExitStack
+
+import concourse.mybir as mybir
+from concourse.masks import make_identity
+
+F32 = mybir.dt.float32
+BF16 = mybir.dt.bfloat16
+U32 = mybir.dt.uint32
+I32 = mybir.dt.int32
+U8 = mybir.dt.uint8
+FP8X4 = mybir.dt.float8_e4m3fn_x4
+FP4X4 = mybir.dt.float4_e2m1fn_x4
+ACT = mybir.ActivationFunctionType
+ALU = mybir.AluOpType
+
+M, K, N = 2048, 1024, 1024
+P = 128
+PACK = 4
+K_PASS = P * PACK
+PASSES = K // K_PASS
+HALF = 512
+TILES = M // P
+FLOOR_SQUARED = 0.0625
+FLOPS = 2 * 2 * M * K * N
+
+S_COLS = 192
+LEFT, RIGHT, WHOLE = slice(0, HALF), slice(HALF, N), slice(0, N)
+V_SUMS = 2
+
+
+def tile_patch_gradient_magnitude_s1_kernel(tc, patches, d_row, d_col_words, d_col_scales, out_0, out_1):
+    nc = tc.nc
+    with ExitStack() as ctx:
+        keep = ctx.enter_context(tc.tile_pool(name="keep", bufs=1))
+        stage = ctx.enter_context(tc.tile_pool(name="stage", bufs=4))
+        work = ctx.enter_context(tc.tile_pool(name="work", bufs=5))
+        outs = ctx.enter_context(tc.tile_pool(name="outs", bufs=5))
+        psum = ctx.enter_context(tc.psum_pool(name="psum", bufs=3))
+        psum_t = ctx.enter_context(tc.psum_pool(name="psum_t", bufs=2))
+
+        ident = keep.tile([P, P], F32)
+        one = keep.tile([P, 1], F32)
+        x_raw = keep.tile([P, TILES, K], BF16, align_bytes=64)
+        dr_raw = keep.tile([P, PASSES, 2, PACK, HALF], BF16, align_bytes=64)
+        dr_grouped = keep.tile([P, PASSES, 2, HALF, PACK], BF16, align_bytes=64)
+        dr_codes = keep.tile([P, PASSES, N], U32, align_bytes=64)
+        dr_scales = keep.tile([P, PASSES, N], U8, align_bytes=64)
+        dc_words = keep.tile([P, PASSES, 2 * N], U8, align_bytes=64)
+        dc_scales = keep.tile([P, PASSES, N], U8, align_bytes=64)
+
+        x_codes, x_scales, x_turned, x_grouped = {}, {}, {}, {}
+        gc_bank, gr_bank, gc_sb, gc_sq, gr_sq, total, diag, mag = {}, {}, {}, {}, {}, {}, {}, {}
+        halves = [(0, 0), (1, 0), (0, 1), (1, 1)] + [(m, h) for m in range(2, TILES) for h in range(2)]
+
+        def load_x(m, count):
+            rows = patches[m * P : (m + count) * P, :].rearrange("(a p) k -> p a k", p=P)
+            nc.sync.dma_start(out=x_raw[:, m : m + count, :], in_=rows)
+
+        def load_d_row(g, h):
+            rows = d_row[g * K_PASS : (g + 1) * K_PASS, h * HALF : (h + 1) * HALF]
+            nc.sync.dma_start(out=dr_raw[:, g, h, :, :], in_=rows.rearrange("(p j) w -> p j w", j=PACK))
+
+        def turn_x(m):
+            xt = psum_t.tile([P, PASSES, 2, P], F32)
+            words = x_raw[:, m, :].bitcast(F32)
+            for g in range(PASSES):
+                for u in range(2):
+                    nc.tensor.transpose(xt[:, g, u, :], words[:, 256 * g + u : 256 * (g + 1) : 2], ident[:])
+            x_turned[m] = xt
+
+        def copy_x(m, on_scalar):
+            grouped = stage.tile([P, PASSES, P, PACK], BF16, align_bytes=64)
+            src = x_turned[m][:].rearrange("p g u r -> p g r u")
+            if on_scalar:
+                nc.scalar.copy(out=grouped[:].bitcast(F32), in_=src)
+            else:
+                nc.vector.tensor_copy(out=grouped[:].bitcast(F32), in_=src)
+            x_grouped[m] = grouped
+
+        def quantize_x(m):
+            codes = stage.tile([P, PASSES * P], U32, align_bytes=64)
+            scales = stage.tile([P, PASSES * P], U8, align_bytes=64)
+            nc.vector.quantize_mx(out=codes[:].bitcast(FP8X4), scales=scales[:], in_=x_grouped[m][:].rearrange("p g r t -> p (g r t)"))
+            x_codes[m], x_scales[m] = codes, scales
+
+        def interleave(g, h):
+            dst = dr_grouped[:, g, h, :, :].rearrange("p (c i) t -> p c t i", i=4)
+            src = dr_raw[:, g, h, :, :].rearrange("p t (c i) -> p c t i", i=4)
+            cut = S_COLS // 4
+            nc.scalar.copy(out=dst[:, :cut], in_=src[:, :cut])
+            nc.vector.tensor_copy(out=dst[:, cut:], in_=src[:, cut:])
+
+        def quantize_d(g, h):
+            cols = slice(h * HALF, (h + 1) * HALF)
+            nc.vector.quantize_mx(
+                out=dr_codes[:, g, cols].bitcast(FP8X4),
+                scales=dr_scales[:, g, cols],
+                in_=dr_grouped[:, g, h, :, :].rearrange("p n t -> p (n t)"),
+            )
+
+        def mm_gc(s):
+            m, h = halves[s]
+            acc_c = psum.tile([P, HALF], F32)
+            for g in range(PASSES):
+                rows = slice(g * P, (g + 1) * P)
+                nc.tensor.matmul_mx(
+                    out=acc_c[:],
+                    lhsT=x_codes[m][:, rows].bitcast(FP8X4),
+                    lhsT_scale=x_scales[m][:, rows],
+                    rhs=dc_words[:, g, 2 * h * HALF : 2 * (h + 1) * HALF].bitcast(FP4X4),
+                    rhs_scale=dc_scales[:, g, h * HALF : (h + 1) * HALF],
+                    start=(g == 0),
+                    stop=(g == PASSES - 1),
+                )
+            gc_bank[s] = acc_c
+
+        def mm_gr(s):
+            m, h = halves[s]
+            acc_r = psum.tile([P, HALF], F32)
+            for g in range(PASSES):
+                rows = slice(g * P, (g + 1) * P)
+                nc.tensor.matmul_mx(
+                    out=acc_r[:],
+                    lhsT=x_codes[m][:, rows].bitcast(FP8X4),
+                    lhsT_scale=x_scales[m][:, rows],
+                    rhs=dr_codes[:, g, h * HALF : (h + 1) * HALF].bitcast(FP8X4),
+                    rhs_scale=dr_scales[:, g, h * HALF : (h + 1) * HALF],
+                    start=(g == 0),
+                    stop=(g == PASSES - 1),
+                )
+            gr_bank[s] = acc_r
+
+        def copy_gc(s):
+            m, h = halves[s]
+            if m not in gc_sb:
+                gc = work.tile([P, N], F32)
+                gc_sb[m] = gc
+            nc.vector.tensor_copy(out=gc_sb[m][:, h * HALF : (h + 1) * HALF], in_=gc_bank[s][:])
+
+        def square_gc(m, cols):
+            if m not in gc_sq:
+                gc2 = work.tile([P, N], F32)
+                gc_sq[m] = gc2
+            nc.scalar.activation(out=gc_sq[m][:, cols], in_=gc_sb[m][:, cols], func=ACT.Square)
+
+        def add_diag(s):
+            m, h = halves[s]
+            if m not in diag:
+                dg = outs.tile([P, N], F32)
+                diag[m] = dg
+            nc.vector.tensor_tensor(out=diag[m][:, h * HALF : (h + 1) * HALF], in0=gr_bank[s][:], in1=gc_sb[m][:, h * HALF : (h + 1) * HALF], op=ALU.add)
+            cols = slice(h * HALF, (h + 1) * HALF)
+            if m >= TILES - 1:
+                nc.sync.dma_start(out=out_1[m * P : (m + 1) * P, cols], in_=diag[m][:, cols])
+            elif h == 1:
+                nc.sync.dma_start(out=out_1[m * P : (m + 1) * P, :], in_=diag[m][:])
+
+        def square_gr(s):
+            gr2 = work.tile([P, HALF], F32)
+            nc.scalar.activation(out=gr2[:], in_=gr_bank[s][:], func=ACT.Square)
+            gr_sq[s] = gr2
+
+        def add_squares(s):
+            m, h = halves[s]
+            cols = slice(h * HALF, (h + 1) * HALF)
+            if m not in total:
+                sm = work.tile([P, N], F32)
+                total[m] = sm
+            eng = nc.vector if s >= len(halves) - V_SUMS else nc.gpsimd
+            eng.tensor_tensor(out=total[m][:, cols], in0=gr_sq[s][:], in1=gc_sq[m][:, cols], op=ALU.add)
+
+        def root(m, cols):
+            if m not in mag:
+                mg = outs.tile([P, N], F32)
+                mag[m] = mg
+            nc.scalar.activation(out=mag[m][:, cols], in_=total[m][:, cols], func=ACT.Sqrt, bias=FLOOR_SQUARED)
+            nc.sync.dma_start(out=out_0[m * P : (m + 1) * P, cols], in_=mag[m][:, cols])
+
+        nc.vector.memset(dc_scales[:].rearrange("p g n -> p (g n)").bitcast(I32), 0)
+        nc.gpsimd.memset(one[:], 1.0)
+        make_identity(nc, ident[:])
+
+        with tc.manual_schedule():
+            load_x(0, 1)
+            for q in range(4):
+                nc.scalar.dma_start(
+                    out=dc_scales[32 * q : 32 * q + 4, :, :].bitcast(I32),
+                    in_=d_col_scales[:, 4 * q : 4 * q + 4, :].rearrange("g r n -> r g n").bitcast(I32),
+                )
+            for g in range(PASSES):
+                nc.sync.dma_start(out=dc_words[:, g, :].bitcast(I32), in_=d_col_words[g].bitcast(I32))
+            load_x(1, 1)
+            load_d_row(0, 0)
+            load_d_row(1, 0)
+            load_d_row(0, 1)
+            load_d_row(1, 1)
+            for m in range(2, TILES, 2):
+                load_x(m, 2)
+
+            warm = keep.tile([P, 1], F32)
+            nc.scalar.activation(out=warm[:], in_=one[:], func=ACT.Sqrt, bias=FLOOR_SQUARED)
+
+            turn_x(0)
+            copy_x(0, False)
+            turn_x(1)
+            copy_x(1, True)
+            quantize_x(0)
+            mm_gc(0)
+            quantize_x(1)
+            mm_gc(1)
+            mm_gc(2)
+            copy_gc(0)
+            square_gc(0, LEFT)
+            copy_gc(1)
+            square_gc(1, LEFT)
+            mm_gc(3)
+            interleave(0, 0)
+            copy_gc(2)
+            quantize_d(0, 0)
+            interleave(1, 0)
+            copy_gc(3)
+            quantize_d(1, 0)
+            square_gc(0, RIGHT)
+            mm_gr(0)
+            mm_gr(1)
+            interleave(0, 1)
+            add_diag(0)
+            square_gr(0)
+            quantize_d(0, 1)
+            interleave(1, 1)
+            add_diag(1)
+            square_gr(1)
+            quantize_d(1, 1)
+            square_gc(1, RIGHT)
+            add_squares(0)
+            add_squares(1)
+            mm_gr(2)
+            mm_gr(3)
+            turn_x(2)
+            turn_x(3)
+            copy_x(2, False)
+            add_diag(2)
+            quantize_x(2)
+            copy_x(3, True)
+            add_diag(3)
+            quantize_x(3)
+            square_gr(2)
+            square_gr(3)
+            add_squares(2)
+            add_squares(3)
+
+            last = len(halves)
+            for s in range(4, last + 1):
+                if s < last:
+                    m, h = halves[s]
+                    mm_gc(s)
+                    mm_gr(s)
+                    if s % 4 == 0 and m + 3 < TILES:
+                        turn_x(m + 2)
+                        turn_x(m + 3)
+                    copy_gc(s)
+                    if m == TILES - 1:
+                        square_gc(m, RIGHT if h else LEFT)
+                    elif h == 1:
+                        square_gc(m, WHOLE)
+                if 5 <= s <= last:
+                    add_diag(s - 1)
+                    square_gr(s - 1)
+                    if s % 2 == 0 and s < last:
+                        add_squares(s - 2)
+                        add_squares(s - 1)
+                if s < last:
+                    pair = s // 4 * 2 + 2
+                    if pair < TILES:
+                        if s % 4 == 1:
+                            copy_x(pair, False)
+                        if s % 4 == 2:
+                            copy_x(pair + 1, False)
+                            quantize_x(pair)
+                        if s % 4 == 3:
+                            quantize_x(pair + 1)
+                if s == 4:
+                    root(0, WHOLE)
+                if s == 5:
+                    root(1, WHOLE)
+                if s % 2 == 0 and 8 <= s < last:
+                    root(s // 2 - 2, WHOLE)
+                if s == last - 1:
+                    root(TILES - 2, WHOLE)
+                if s == last:
+                    add_squares(last - 2)
+                    root(TILES - 1, LEFT)
+                    add_squares(last - 1)
+                    root(TILES - 1, RIGHT)

@@ -23,9 +23,8 @@ TILES = M // P
 FLOOR_SQUARED = 0.0625
 FLOPS = 2 * 2 * M * K * N
 
-S_COLS = 192
+S_COLS = 256
 LEFT, RIGHT, WHOLE = slice(0, HALF), slice(HALF, N), slice(0, N)
-V_SUMS = 2
 
 
 def tile_patch_gradient_magnitude_s1_kernel(tc, patches, d_row, d_col_words, d_col_scales, out_0, out_1):
@@ -50,7 +49,6 @@ def tile_patch_gradient_magnitude_s1_kernel(tc, patches, d_row, d_col_words, d_c
 
         x_codes, x_scales, x_turned, x_grouped = {}, {}, {}, {}
         gc_bank, gr_bank, gc_sb, gc_sq, gr_sq, total, diag, mag = {}, {}, {}, {}, {}, {}, {}, {}
-        halves = [(0, 0), (1, 0), (0, 1), (1, 1)] + [(m, h) for m in range(2, TILES) for h in range(2)]
 
         def load_x(m, count):
             rows = patches[m * P : (m + count) * P, :].rearrange("(a p) k -> p a k", p=P)
@@ -99,7 +97,7 @@ def tile_patch_gradient_magnitude_s1_kernel(tc, patches, d_row, d_col_words, d_c
             )
 
         def mm_gc(s):
-            m, h = halves[s]
+            m, h = s
             acc_c = psum.tile([P, HALF], F32)
             for g in range(PASSES):
                 rows = slice(g * P, (g + 1) * P)
@@ -115,7 +113,7 @@ def tile_patch_gradient_magnitude_s1_kernel(tc, patches, d_row, d_col_words, d_c
             gc_bank[s] = acc_c
 
         def mm_gr(s):
-            m, h = halves[s]
+            m, h = s
             acc_r = psum.tile([P, HALF], F32)
             for g in range(PASSES):
                 rows = slice(g * P, (g + 1) * P)
@@ -131,7 +129,7 @@ def tile_patch_gradient_magnitude_s1_kernel(tc, patches, d_row, d_col_words, d_c
             gr_bank[s] = acc_r
 
         def copy_gc(s):
-            m, h = halves[s]
+            m, h = s
             if m not in gc_sb:
                 gc = work.tile([P, N], F32)
                 gc_sb[m] = gc
@@ -144,13 +142,13 @@ def tile_patch_gradient_magnitude_s1_kernel(tc, patches, d_row, d_col_words, d_c
             nc.scalar.activation(out=gc_sq[m][:, cols], in_=gc_sb[m][:, cols], func=ACT.Square)
 
         def add_diag(s):
-            m, h = halves[s]
+            m, h = s
             if m not in diag:
                 dg = outs.tile([P, N], F32)
                 diag[m] = dg
             nc.vector.tensor_tensor(out=diag[m][:, h * HALF : (h + 1) * HALF], in0=gr_bank[s][:], in1=gc_sb[m][:, h * HALF : (h + 1) * HALF], op=ALU.add)
             cols = slice(h * HALF, (h + 1) * HALF)
-            if m >= TILES - 1:
+            if m == TILES - 1:
                 nc.sync.dma_start(out=out_1[m * P : (m + 1) * P, cols], in_=diag[m][:, cols])
             elif h == 1:
                 nc.sync.dma_start(out=out_1[m * P : (m + 1) * P, :], in_=diag[m][:])
@@ -160,13 +158,13 @@ def tile_patch_gradient_magnitude_s1_kernel(tc, patches, d_row, d_col_words, d_c
             nc.scalar.activation(out=gr2[:], in_=gr_bank[s][:], func=ACT.Square)
             gr_sq[s] = gr2
 
-        def add_squares(s):
-            m, h = halves[s]
+        def add_squares(s, on_vector=False):
+            m, h = s
             cols = slice(h * HALF, (h + 1) * HALF)
             if m not in total:
                 sm = work.tile([P, N], F32)
                 total[m] = sm
-            eng = nc.vector if s >= len(halves) - V_SUMS else nc.gpsimd
+            eng = nc.vector if on_vector else nc.gpsimd
             eng.tensor_tensor(out=total[m][:, cols], in0=gr_sq[s][:], in1=gc_sq[m][:, cols], op=ALU.add)
 
         def root(m, cols):
@@ -182,6 +180,8 @@ def tile_patch_gradient_magnitude_s1_kernel(tc, patches, d_row, d_col_words, d_c
 
         with tc.manual_schedule():
             load_x(0, 1)
+            load_x(1, 1)
+            load_d_row(0, 0)
             for q in range(4):
                 nc.scalar.dma_start(
                     out=dc_scales[32 * q : 32 * q + 4, :, :].bitcast(I32),
@@ -189,8 +189,6 @@ def tile_patch_gradient_magnitude_s1_kernel(tc, patches, d_row, d_col_words, d_c
                 )
             for g in range(PASSES):
                 nc.sync.dma_start(out=dc_words[:, g, :].bitcast(I32), in_=d_col_words[g].bitcast(I32))
-            load_x(1, 1)
-            load_d_row(0, 0)
             load_d_row(1, 0)
             load_d_row(0, 1)
             load_d_row(1, 1)
@@ -200,95 +198,85 @@ def tile_patch_gradient_magnitude_s1_kernel(tc, patches, d_row, d_col_words, d_c
             warm = keep.tile([P, 1], F32)
             nc.scalar.activation(out=warm[:], in_=one[:], func=ACT.Sqrt, bias=FLOOR_SQUARED)
 
+            L0, L1, R0, R1 = (0, 0), (1, 0), (0, 1), (1, 1)
             turn_x(0)
-            copy_x(0, False)
             turn_x(1)
+            copy_x(0, False)
             copy_x(1, True)
-            quantize_x(0)
-            mm_gc(0)
-            quantize_x(1)
-            mm_gc(1)
-            mm_gc(2)
-            copy_gc(0)
-            square_gc(0, LEFT)
-            copy_gc(1)
-            square_gc(1, LEFT)
-            mm_gc(3)
             interleave(0, 0)
-            copy_gc(2)
+            quantize_x(0)
+            mm_gc(L0)
+            quantize_x(1)
+            mm_gc(L1)
+            mm_gc(R0)
+            copy_gc(L0)
             quantize_d(0, 0)
             interleave(1, 0)
-            copy_gc(3)
+            copy_gc(L1)
+            mm_gc(R1)
+            square_gc(0, LEFT)
             quantize_d(1, 0)
-            square_gc(0, RIGHT)
-            mm_gr(0)
-            mm_gr(1)
-            interleave(0, 1)
-            add_diag(0)
-            square_gr(0)
-            quantize_d(0, 1)
-            interleave(1, 1)
-            add_diag(1)
-            square_gr(1)
-            quantize_d(1, 1)
-            square_gc(1, RIGHT)
-            add_squares(0)
-            add_squares(1)
-            mm_gr(2)
-            mm_gr(3)
+            mm_gr(L0)
+            mm_gr(L1)
             turn_x(2)
             turn_x(3)
+            interleave(0, 1)
+            add_diag(L0)
+            copy_gc(R0)
+            quantize_d(0, 1)
+            interleave(1, 1)
+            square_gr(L0)
+            square_gc(1, LEFT)
+            add_diag(L1)
+            square_gr(L1)
+            copy_gc(R1)
+            square_gc(0, RIGHT)
+            quantize_d(1, 1)
+            mm_gr(R0)
+            mm_gr(R1)
             copy_x(2, False)
-            add_diag(2)
+            square_gc(1, RIGHT)
+            add_squares(L0)
             quantize_x(2)
-            copy_x(3, True)
-            add_diag(3)
-            quantize_x(3)
-            square_gr(2)
-            square_gr(3)
-            add_squares(2)
-            add_squares(3)
+            add_diag(R0)
+            copy_x(3, False)
+            square_gr(R0)
+            add_squares(R0)
 
-            last = len(halves)
-            for s in range(4, last + 1):
-                if s < last:
-                    m, h = halves[s]
-                    mm_gc(s)
-                    mm_gr(s)
-                    if s % 4 == 0 and m + 3 < TILES:
-                        turn_x(m + 2)
-                        turn_x(m + 3)
-                    copy_gc(s)
-                    if m == TILES - 1:
-                        square_gc(m, RIGHT if h else LEFT)
-                    elif h == 1:
-                        square_gc(m, WHOLE)
-                if 5 <= s <= last:
-                    add_diag(s - 1)
-                    square_gr(s - 1)
-                    if s % 2 == 0 and s < last:
-                        add_squares(s - 2)
-                        add_squares(s - 1)
-                if s < last:
-                    pair = s // 4 * 2 + 2
-                    if pair < TILES:
-                        if s % 4 == 1:
-                            copy_x(pair, False)
-                        if s % 4 == 2:
-                            copy_x(pair + 1, False)
-                            quantize_x(pair)
-                        if s % 4 == 3:
-                            quantize_x(pair + 1)
-                if s == 4:
-                    root(0, WHOLE)
-                if s == 5:
-                    root(1, WHOLE)
-                if s % 2 == 0 and 8 <= s < last:
-                    root(s // 2 - 2, WHOLE)
-                if s == last - 1:
-                    root(TILES - 2, WHOLE)
-                if s == last:
-                    add_squares(last - 2)
-                    root(TILES - 1, LEFT)
-                    add_squares(last - 1)
-                    root(TILES - 1, RIGHT)
+            for m in range(2, TILES):
+                last = m == TILES - 1
+                left, right, before = (m, 0), (m, 1), (m - 1, 1)
+                mm_gc(left)
+                mm_gr(left)
+                mm_gc(right)
+                mm_gr(right)
+                if m % 2 == 0 and m + 3 < TILES:
+                    turn_x(m + 2)
+                    turn_x(m + 3)
+                copy_gc(left)
+                if m + 1 < TILES:
+                    quantize_x(m + 1)
+                root(m - 2, WHOLE)
+                add_diag(before)
+                square_gr(before)
+                add_squares((m - 1, 0))
+                if not last:
+                    add_squares(before)
+                if last:
+                    square_gc(m, LEFT)
+                copy_gc(right)
+                square_gc(m, RIGHT if last else WHOLE)
+                if last:
+                    add_squares(before, True)
+                add_diag(left)
+                square_gr(left)
+                if m + 2 < TILES:
+                    copy_x(m + 2, False)
+            left, right = (TILES - 1, 0), (TILES - 1, 1)
+            square_gr(right)
+            add_squares(left, True)
+            root(TILES - 2, WHOLE)
+            root(TILES - 1, LEFT)
+            add_squares(right, True)
+            root(TILES - 1, RIGHT)
+            add_diag(right)

@@ -22,23 +22,23 @@ HALF = 512
 TILES = M // P
 FLOOR_SQUARED = 0.0625
 FLOPS = 2 * 2 * M * K * N
-
 S_COLS = 256
-LEFT, RIGHT, WHOLE = slice(0, HALF), slice(HALF, N), slice(0, N)
+L, R, W = slice(0, HALF), slice(HALF, N), slice(0, N)
 
 
 def tile_patch_gradient_magnitude_s1_kernel(tc, patches, d_row, d_col_words, d_col_scales, out_0, out_1):
     nc = tc.nc
     with ExitStack() as ctx:
         keep = ctx.enter_context(tc.tile_pool(name="keep", bufs=1))
-        stage = ctx.enter_context(tc.tile_pool(name="stage", bufs=4))
-        work = ctx.enter_context(tc.tile_pool(name="work", bufs=5))
+        stage = ctx.enter_context(tc.tile_pool(name="stage", bufs=3))
+        work = ctx.enter_context(tc.tile_pool(name="work", bufs=4))
         outs = ctx.enter_context(tc.tile_pool(name="outs", bufs=5))
         psum = ctx.enter_context(tc.psum_pool(name="psum", bufs=3))
         psum_t = ctx.enter_context(tc.psum_pool(name="psum_t", bufs=2))
 
         ident = keep.tile([P, P], F32)
         one = keep.tile([P, 1], F32)
+        warm = keep.tile([P, 1], F32)
         x_raw = keep.tile([P, TILES, K], BF16, align_bytes=64)
         dr_raw = keep.tile([P, PASSES, 2, PACK, HALF], BF16, align_bytes=64)
         dr_grouped = keep.tile([P, PASSES, 2, HALF, PACK], BF16, align_bytes=64)
@@ -49,6 +49,7 @@ def tile_patch_gradient_magnitude_s1_kernel(tc, patches, d_row, d_col_words, d_c
 
         x_codes, x_scales, x_turned, x_grouped = {}, {}, {}, {}
         gc_bank, gr_bank, gc_sb, gc_sq, gr_sq, total, diag, mag = {}, {}, {}, {}, {}, {}, {}, {}
+        engines = {"S": nc.scalar, "V": nc.vector, "G": nc.gpsimd}
 
         def load_x(m, count):
             rows = patches[m * P : (m + count) * P, :].rearrange("(a p) k -> p a k", p=P)
@@ -58,7 +59,17 @@ def tile_patch_gradient_magnitude_s1_kernel(tc, patches, d_row, d_col_words, d_c
             rows = d_row[g * K_PASS : (g + 1) * K_PASS, h * HALF : (h + 1) * HALF]
             nc.sync.dma_start(out=dr_raw[:, g, h, :, :], in_=rows.rearrange("(p j) w -> p j w", j=PACK))
 
-        def turn_x(m):
+        def load_words(g):
+            nc.sync.dma_start(out=dc_words[:, g, :].bitcast(I32), in_=d_col_words[g].bitcast(I32))
+
+        def load_scales():
+            for q in range(4):
+                nc.scalar.dma_start(
+                    out=dc_scales[32 * q : 32 * q + 4, :, :].bitcast(I32),
+                    in_=d_col_scales[:, 4 * q : 4 * q + 4, :].rearrange("g r n -> r g n").bitcast(I32),
+                )
+
+        def turn(m):
             xt = psum_t.tile([P, PASSES, 2, P], F32)
             words = x_raw[:, m, :].bitcast(F32)
             for g in range(PASSES):
@@ -66,29 +77,35 @@ def tile_patch_gradient_magnitude_s1_kernel(tc, patches, d_row, d_col_words, d_c
                     nc.tensor.transpose(xt[:, g, u, :], words[:, 256 * g + u : 256 * (g + 1) : 2], ident[:])
             x_turned[m] = xt
 
-        def copy_x(m, on_scalar):
-            grouped = stage.tile([P, PASSES, P, PACK], BF16, align_bytes=64)
+        def copy_x(m, e):
+            if m // 2 not in x_grouped:
+                grouped = stage.tile([P, 2, PASSES, P, PACK], BF16, align_bytes=64)
+                codes = stage.tile([P, 2, PASSES * P], U32, align_bytes=64)
+                scales = stage.tile([P, 2, PASSES * P], U8, align_bytes=64)
+                x_grouped[m // 2], x_codes[m // 2], x_scales[m // 2] = grouped, codes, scales
+            dst = x_grouped[m // 2][:, m % 2, :, :, :].bitcast(F32)
             src = x_turned[m][:].rearrange("p g u r -> p g r u")
-            if on_scalar:
-                nc.scalar.copy(out=grouped[:].bitcast(F32), in_=src)
+            if e == "S":
+                nc.scalar.copy(out=dst, in_=src)
             else:
-                nc.vector.tensor_copy(out=grouped[:].bitcast(F32), in_=src)
-            x_grouped[m] = grouped
+                nc.vector.tensor_copy(out=dst, in_=src)
 
-        def quantize_x(m):
-            codes = stage.tile([P, PASSES * P], U32, align_bytes=64)
-            scales = stage.tile([P, PASSES * P], U8, align_bytes=64)
-            nc.vector.quantize_mx(out=codes[:].bitcast(FP8X4), scales=scales[:], in_=x_grouped[m][:].rearrange("p g r t -> p (g r t)"))
-            x_codes[m], x_scales[m] = codes, scales
+        def quant_x(m, count=1):
+            pair, a, b = m // 2, m % 2, m % 2 + count
+            nc.vector.quantize_mx(
+                out=x_codes[pair][:, a:b, :].rearrange("p a w -> p (a w)").bitcast(FP8X4),
+                scales=x_scales[pair][:, a:b, :].rearrange("p a w -> p (a w)"),
+                in_=x_grouped[pair][:, a:b, :, :, :].rearrange("p a g r t -> p (a g r t)"),
+            )
 
-        def interleave(g, h):
+        def inter(g, h):
             dst = dr_grouped[:, g, h, :, :].rearrange("p (c i) t -> p c t i", i=4)
             src = dr_raw[:, g, h, :, :].rearrange("p t (c i) -> p c t i", i=4)
             cut = S_COLS // 4
             nc.scalar.copy(out=dst[:, :cut], in_=src[:, :cut])
             nc.vector.tensor_copy(out=dst[:, cut:], in_=src[:, cut:])
 
-        def quantize_d(g, h):
+        def quant_d(g, h):
             cols = slice(h * HALF, (h + 1) * HALF)
             nc.vector.quantize_mx(
                 out=dr_codes[:, g, cols].bitcast(FP8X4),
@@ -96,76 +113,69 @@ def tile_patch_gradient_magnitude_s1_kernel(tc, patches, d_row, d_col_words, d_c
                 in_=dr_grouped[:, g, h, :, :].rearrange("p n t -> p (n t)"),
             )
 
-        def mm_gc(s):
-            m, h = s
+        def product(acc, m, words, scales):
+            for g in range(PASSES):
+                rows = slice(g * P, (g + 1) * P)
+                nc.tensor.matmul_mx(
+                    out=acc[:],
+                    lhsT=x_codes[m // 2][:, m % 2, rows].bitcast(FP8X4),
+                    lhsT_scale=x_scales[m // 2][:, m % 2, rows],
+                    rhs=words(g),
+                    rhs_scale=scales[g],
+                    start=(g == 0),
+                    stop=(g == PASSES - 1),
+                )
+
+        def mm_gc(m, h):
             acc_c = psum.tile([P, HALF], F32)
-            for g in range(PASSES):
-                rows = slice(g * P, (g + 1) * P)
-                nc.tensor.matmul_mx(
-                    out=acc_c[:],
-                    lhsT=x_codes[m][:, rows].bitcast(FP8X4),
-                    lhsT_scale=x_scales[m][:, rows],
-                    rhs=dc_words[:, g, 2 * h * HALF : 2 * (h + 1) * HALF].bitcast(FP4X4),
-                    rhs_scale=dc_scales[:, g, h * HALF : (h + 1) * HALF],
-                    start=(g == 0),
-                    stop=(g == PASSES - 1),
-                )
-            gc_bank[s] = acc_c
+            cols = slice(h * HALF, (h + 1) * HALF)
+            product(acc_c, m, lambda g: dc_words[:, g, 2 * h * HALF : 2 * (h + 1) * HALF].bitcast(FP4X4), [dc_scales[:, g, cols] for g in range(PASSES)])
+            gc_bank[m, h] = acc_c
 
-        def mm_gr(s):
-            m, h = s
+        def mm_gr(m, h):
             acc_r = psum.tile([P, HALF], F32)
-            for g in range(PASSES):
-                rows = slice(g * P, (g + 1) * P)
-                nc.tensor.matmul_mx(
-                    out=acc_r[:],
-                    lhsT=x_codes[m][:, rows].bitcast(FP8X4),
-                    lhsT_scale=x_scales[m][:, rows],
-                    rhs=dr_codes[:, g, h * HALF : (h + 1) * HALF].bitcast(FP8X4),
-                    rhs_scale=dr_scales[:, g, h * HALF : (h + 1) * HALF],
-                    start=(g == 0),
-                    stop=(g == PASSES - 1),
-                )
-            gr_bank[s] = acc_r
+            cols = slice(h * HALF, (h + 1) * HALF)
+            product(acc_r, m, lambda g: dr_codes[:, g, cols].bitcast(FP8X4), [dr_scales[:, g, cols] for g in range(PASSES)])
+            gr_bank[m, h] = acc_r
 
-        def copy_gc(s):
-            m, h = s
+        def copy_gc(m, h):
             if m not in gc_sb:
                 gc = work.tile([P, N], F32)
                 gc_sb[m] = gc
-            nc.vector.tensor_copy(out=gc_sb[m][:, h * HALF : (h + 1) * HALF], in_=gc_bank[s][:])
+            nc.vector.tensor_copy(out=gc_sb[m][:, h * HALF : (h + 1) * HALF], in_=gc_bank[m, h][:])
 
-        def square_gc(m, cols):
+        def square_gc(m, cols, e="S"):
             if m not in gc_sq:
                 gc2 = work.tile([P, N], F32)
                 gc_sq[m] = gc2
-            nc.scalar.activation(out=gc_sq[m][:, cols], in_=gc_sb[m][:, cols], func=ACT.Square)
+            gc = gc_sb[m][:, cols]
+            if e == "S":
+                nc.scalar.activation(out=gc_sq[m][:, cols], in_=gc, func=ACT.Square)
+            else:
+                engines[e].tensor_tensor(out=gc_sq[m][:, cols], in0=gc, in1=gc, op=ALU.mult)
 
-        def add_diag(s):
-            m, h = s
+        def diagonal(m, h):
             if m not in diag:
                 dg = outs.tile([P, N], F32)
                 diag[m] = dg
-            nc.vector.tensor_tensor(out=diag[m][:, h * HALF : (h + 1) * HALF], in0=gr_bank[s][:], in1=gc_sb[m][:, h * HALF : (h + 1) * HALF], op=ALU.add)
             cols = slice(h * HALF, (h + 1) * HALF)
+            nc.vector.tensor_tensor(out=diag[m][:, cols], in0=gr_bank[m, h][:], in1=gc_sb[m][:, cols], op=ALU.add)
             if m == TILES - 1:
                 nc.sync.dma_start(out=out_1[m * P : (m + 1) * P, cols], in_=diag[m][:, cols])
             elif h == 1:
                 nc.sync.dma_start(out=out_1[m * P : (m + 1) * P, :], in_=diag[m][:])
 
-        def square_gr(s):
-            gr2 = work.tile([P, HALF], F32)
-            nc.scalar.activation(out=gr2[:], in_=gr_bank[s][:], func=ACT.Square)
-            gr_sq[s] = gr2
+        def square_gr(m, h):
+            if m not in gr_sq:
+                gr2 = work.tile([P, N], F32)
+                gr_sq[m] = gr2
+            nc.scalar.activation(out=gr_sq[m][:, h * HALF : (h + 1) * HALF], in_=gr_bank[m, h][:], func=ACT.Square)
 
-        def add_squares(s, on_vector=False):
-            m, h = s
-            cols = slice(h * HALF, (h + 1) * HALF)
+        def add_squares(m, cols, e="G"):
             if m not in total:
                 sm = work.tile([P, N], F32)
                 total[m] = sm
-            eng = nc.vector if on_vector else nc.gpsimd
-            eng.tensor_tensor(out=total[m][:, cols], in0=gr_sq[s][:], in1=gc_sq[m][:, cols], op=ALU.add)
+            engines[e].tensor_tensor(out=total[m][:, cols], in0=gr_sq[m][:, cols], in1=gc_sq[m][:, cols], op=ALU.add)
 
         def root(m, cols):
             if m not in mag:
@@ -179,104 +189,130 @@ def tile_patch_gradient_magnitude_s1_kernel(tc, patches, d_row, d_col_words, d_c
         make_identity(nc, ident[:])
 
         with tc.manual_schedule():
-            load_x(0, 1)
-            load_x(1, 1)
             load_d_row(0, 0)
-            for q in range(4):
-                nc.scalar.dma_start(
-                    out=dc_scales[32 * q : 32 * q + 4, :, :].bitcast(I32),
-                    in_=d_col_scales[:, 4 * q : 4 * q + 4, :].rearrange("g r n -> r g n").bitcast(I32),
-                )
-            for g in range(PASSES):
-                nc.sync.dma_start(out=dc_words[:, g, :].bitcast(I32), in_=d_col_words[g].bitcast(I32))
+            load_x(0, 1)
             load_d_row(1, 0)
+            load_x(1, 1)
             load_d_row(0, 1)
+            load_scales()
+            load_words(0)
+            load_words(1)
             load_d_row(1, 1)
-            for m in range(2, TILES, 2):
-                load_x(m, 2)
-
-            warm = keep.tile([P, 1], F32)
+            load_x(2, 2)
+            load_x(4, 2)
+            load_x(6, 2)
+            load_x(8, 2)
+            load_x(10, 2)
+            load_x(12, 2)
+            load_x(14, 2)
             nc.scalar.activation(out=warm[:], in_=one[:], func=ACT.Sqrt, bias=FLOOR_SQUARED)
-
-            L0, L1, R0, R1 = (0, 0), (1, 0), (0, 1), (1, 1)
-            turn_x(0)
-            turn_x(1)
-            copy_x(0, False)
-            copy_x(1, True)
-            interleave(0, 0)
-            quantize_x(0)
-            mm_gc(L0)
-            quantize_x(1)
-            mm_gc(L1)
-            mm_gc(R0)
-            copy_gc(L0)
-            quantize_d(0, 0)
-            interleave(1, 0)
-            copy_gc(L1)
-            mm_gc(R1)
-            square_gc(0, LEFT)
-            quantize_d(1, 0)
-            mm_gr(L0)
-            mm_gr(L1)
-            turn_x(2)
-            turn_x(3)
-            interleave(0, 1)
-            add_diag(L0)
-            copy_gc(R0)
-            quantize_d(0, 1)
-            interleave(1, 1)
-            square_gr(L0)
-            square_gc(1, LEFT)
-            add_diag(L1)
-            square_gr(L1)
-            copy_gc(R1)
-            square_gc(0, RIGHT)
-            quantize_d(1, 1)
-            mm_gr(R0)
-            mm_gr(R1)
-            copy_x(2, False)
-            square_gc(1, RIGHT)
-            add_squares(L0)
-            quantize_x(2)
-            add_diag(R0)
-            copy_x(3, False)
-            square_gr(R0)
-            add_squares(R0)
-
-            for m in range(2, TILES):
-                last = m == TILES - 1
-                left, right, before = (m, 0), (m, 1), (m - 1, 1)
-                mm_gc(left)
-                mm_gr(left)
-                mm_gc(right)
-                mm_gr(right)
-                if m % 2 == 0 and m + 3 < TILES:
-                    turn_x(m + 2)
-                    turn_x(m + 3)
-                copy_gc(left)
-                if m + 1 < TILES:
-                    quantize_x(m + 1)
-                root(m - 2, WHOLE)
-                add_diag(before)
-                square_gr(before)
-                add_squares((m - 1, 0))
-                if not last:
-                    add_squares(before)
-                if last:
-                    square_gc(m, LEFT)
-                copy_gc(right)
-                square_gc(m, RIGHT if last else WHOLE)
-                if last:
-                    add_squares(before, True)
-                add_diag(left)
-                square_gr(left)
-                if m + 2 < TILES:
-                    copy_x(m + 2, False)
-            left, right = (TILES - 1, 0), (TILES - 1, 1)
-            square_gr(right)
-            add_squares(left, True)
-            root(TILES - 2, WHOLE)
-            root(TILES - 1, LEFT)
-            add_squares(right, True)
-            root(TILES - 1, RIGHT)
-            add_diag(right)
+            turn(0)
+            inter(0, 0)
+            copy_x(0, "V")
+            inter(1, 0)
+            quant_x(0)
+            turn(1)
+            copy_x(1, "S")
+            quant_d(0, 0)
+            inter(0, 1)
+            quant_x(1)
+            mm_gc(0, 0)
+            mm_gc(0, 1)
+            quant_d(1, 0)
+            copy_gc(0, 0)
+            copy_gc(0, 1)
+            mm_gr(0, 0)
+            square_gc(0, R, "G")
+            inter(1, 1)
+            mm_gr(1, 0)
+            quant_d(0, 1)
+            mm_gc(1, 0)
+            turn(3)
+            quant_d(1, 1)
+            square_gr(1, 0)
+            square_gc(0, L, "S")
+            turn(2)
+            diagonal(0, 0)
+            copy_x(3, "S")
+            mm_gc(1, 1)
+            mm_gr(0, 1)
+            copy_gc(1, 0)
+            copy_x(2, "S")
+            square_gr(0, 0)
+            copy_gc(1, 1)
+            square_gr(0, 1)
+            mm_gr(1, 1)
+            quant_x(2, 2)
+            square_gc(1, L, "S")
+            diagonal(1, 0)
+            add_squares(0, W, "G")
+            square_gc(1, R, "S")
+            diagonal(0, 1)
+            for m in range(2, TILES - 2, 2):
+                mm_gc(m, 0)
+                mm_gr(m, 1)
+                mm_gc(m, 1)
+                diagonal(m - 1, 1)
+                square_gr(m - 1, 1)
+                root(m - 2, W)
+                copy_gc(m, 0)
+                mm_gr(m, 0)
+                mm_gc(m + 1, 0)
+                copy_gc(m, 1)
+                square_gc(m, W, "S")
+                diagonal(m, 0)
+                diagonal(m, 1)
+                turn(m + 2)
+                turn(m + 3)
+                copy_x(m + 2, "V")
+                square_gr(m, 1)
+                square_gr(m, 0)
+                add_squares(m - 1, W, "G")
+                mm_gr(m + 1, 0)
+                copy_x(m + 3, "V")
+                mm_gc(m + 1, 1)
+                copy_gc(m + 1, 0)
+                square_gr(m + 1, 0)
+                quant_x(m + 2, 2)
+                copy_gc(m + 1, 1)
+                diagonal(m + 1, 0)
+                add_squares(m, W, "G")
+                root(m - 1, W)
+                mm_gr(m + 1, 1)
+                square_gc(m + 1, R, "G")
+                square_gc(m + 1, L, "S")
+            mm_gc(14, 0)
+            mm_gr(15, 0)
+            square_gr(13, 1)
+            copy_gc(14, 0)
+            mm_gc(15, 1)
+            mm_gc(14, 1)
+            add_squares(13, W, "G")
+            mm_gc(15, 0)
+            copy_gc(15, 1)
+            copy_gc(14, 1)
+            mm_gr(14, 0)
+            diagonal(13, 1)
+            root(12, W)
+            square_gc(14, W, "S")
+            mm_gr(14, 1)
+            square_gr(14, 0)
+            copy_gc(15, 0)
+            square_gr(14, 1)
+            diagonal(15, 0)
+            square_gc(15, L, "V")
+            diagonal(14, 0)
+            square_gr(15, 0)
+            diagonal(14, 1)
+            add_squares(15, L, "V")
+            root(13, W)
+            add_squares(14, L, "G")
+            mm_gr(15, 1)
+            add_squares(14, R, "G")
+            root(15, L)
+            diagonal(15, 1)
+            square_gc(15, R, "V")
+            square_gr(15, 1)
+            root(14, W)
+            add_squares(15, R, "V")
+            root(15, R)

@@ -23,6 +23,7 @@ TILES = M // P
 FLOOR_SQUARED = 0.0625
 FLOPS = 2 * 2 * M * K * N
 S_COLS = 256
+GCB, GRB = 3, 3
 L, R, W = slice(0, HALF), slice(HALF, N), slice(0, N)
 
 
@@ -51,9 +52,12 @@ def tile_patch_gradient_magnitude_s1_kernel(tc, patches, d_row, d_col_words, d_c
         gc_bank, gr_bank, gc_sb, gc_sq, gr_sq, total, diag, mag = {}, {}, {}, {}, {}, {}, {}, {}
         engines = {"S": nc.scalar, "V": nc.vector, "G": nc.gpsimd}
 
+        def pair_rows(tensor, m):
+            first = m // 2 * 2 * P
+            return tensor[first : first + 2 * P, :].rearrange("(p a) k -> p a k", a=2)
+
         def load_x(m, count):
-            rows = patches[m * P : (m + count) * P, :].rearrange("(a p) k -> p a k", p=P)
-            nc.sync.dma_start(out=x_raw[:, m : m + count, :], in_=rows)
+            nc.sync.dma_start(out=x_raw[:, m : m + count, :], in_=pair_rows(patches, m)[:, m % 2 : m % 2 + count, :])
 
         def load_d_row(g, h):
             rows = d_row[g * K_PASS : (g + 1) * K_PASS, h * HALF : (h + 1) * HALF]
@@ -64,7 +68,7 @@ def tile_patch_gradient_magnitude_s1_kernel(tc, patches, d_row, d_col_words, d_c
 
         def load_scales():
             for q in range(4):
-                nc.scalar.dma_start(
+                nc.sync.dma_start(
                     out=dc_scales[32 * q : 32 * q + 4, :, :].bitcast(I32),
                     in_=d_col_scales[:, 4 * q : 4 * q + 4, :].rearrange("g r n -> r g n").bitcast(I32),
                 )
@@ -98,11 +102,14 @@ def tile_patch_gradient_magnitude_s1_kernel(tc, patches, d_row, d_col_words, d_c
                 in_=x_grouped[pair][:, a:b, :, :, :].rearrange("p a g r t -> p (a g r t)"),
             )
 
-        def inter(g, h):
+        def inter(g, h, e="S"):
             dst = dr_grouped[:, g, h, :, :].rearrange("p (c i) t -> p c t i", i=4)
             src = dr_raw[:, g, h, :, :].rearrange("p t (c i) -> p c t i", i=4)
             cut = S_COLS // 4
-            nc.scalar.copy(out=dst[:, :cut], in_=src[:, :cut])
+            if e == "S":
+                nc.scalar.copy(out=dst[:, :cut], in_=src[:, :cut])
+            else:
+                nc.gpsimd.tensor_scalar(out=dst[:, :cut], in0=src[:, :cut], scalar1=1.0, scalar2=0.0, op0=ALU.mult, op1=ALU.add)
             nc.vector.tensor_copy(out=dst[:, cut:], in_=src[:, cut:])
 
         def quant_d(g, h):
@@ -127,13 +134,13 @@ def tile_patch_gradient_magnitude_s1_kernel(tc, patches, d_row, d_col_words, d_c
                 )
 
         def mm_gc(m, h):
-            acc_c = psum.tile([P, HALF], F32)
+            acc_c = psum.tile([P, HALF], F32, bufs=GCB)
             cols = slice(h * HALF, (h + 1) * HALF)
             product(acc_c, m, lambda g: dc_words[:, g, 2 * h * HALF : 2 * (h + 1) * HALF].bitcast(FP4X4), [dc_scales[:, g, cols] for g in range(PASSES)])
             gc_bank[m, h] = acc_c
 
         def mm_gr(m, h):
-            acc_r = psum.tile([P, HALF], F32)
+            acc_r = psum.tile([P, HALF], F32, bufs=GRB)
             cols = slice(h * HALF, (h + 1) * HALF)
             product(acc_r, m, lambda g: dr_codes[:, g, cols].bitcast(FP8X4), [dr_scales[:, g, cols] for g in range(PASSES)])
             gr_bank[m, h] = acc_r
@@ -161,9 +168,9 @@ def tile_patch_gradient_magnitude_s1_kernel(tc, patches, d_row, d_col_words, d_c
             cols = slice(h * HALF, (h + 1) * HALF)
             nc.vector.tensor_tensor(out=diag[m][:, cols], in0=gr_bank[m, h][:], in1=gc_sb[m][:, cols], op=ALU.add)
             if m == TILES - 1:
-                nc.sync.dma_start(out=out_1[m * P : (m + 1) * P, cols], in_=diag[m][:, cols])
+                nc.sync.dma_start(out=pair_rows(out_1, m)[:, m % 2, cols], in_=diag[m][:, cols])
             elif h == 1:
-                nc.sync.dma_start(out=out_1[m * P : (m + 1) * P, :], in_=diag[m][:])
+                nc.sync.dma_start(out=pair_rows(out_1, m)[:, m % 2, :], in_=diag[m][:])
 
         def square_gr(m, h):
             if m not in gr_sq:
@@ -182,21 +189,21 @@ def tile_patch_gradient_magnitude_s1_kernel(tc, patches, d_row, d_col_words, d_c
                 mg = outs.tile([P, N], F32)
                 mag[m] = mg
             nc.scalar.activation(out=mag[m][:, cols], in_=total[m][:, cols], func=ACT.Sqrt, bias=FLOOR_SQUARED)
-            nc.sync.dma_start(out=out_0[m * P : (m + 1) * P, cols], in_=mag[m][:, cols])
+            nc.sync.dma_start(out=pair_rows(out_0, m)[:, m % 2, cols], in_=mag[m][:, cols])
 
         nc.vector.memset(dc_scales[:].rearrange("p g n -> p (g n)").bitcast(I32), 0)
         nc.gpsimd.memset(one[:], 1.0)
         make_identity(nc, ident[:])
 
         with tc.manual_schedule():
-            load_d_row(0, 0)
             load_x(0, 1)
             load_d_row(1, 0)
-            load_x(1, 1)
-            load_d_row(0, 1)
+            load_d_row(0, 0)
             load_scales()
+            load_x(1, 1)
             load_words(0)
             load_words(1)
+            load_d_row(0, 1)
             load_d_row(1, 1)
             load_x(2, 2)
             load_x(4, 2)
@@ -207,112 +214,112 @@ def tile_patch_gradient_magnitude_s1_kernel(tc, patches, d_row, d_col_words, d_c
             load_x(14, 2)
             nc.scalar.activation(out=warm[:], in_=one[:], func=ACT.Sqrt, bias=FLOOR_SQUARED)
             turn(0)
-            inter(0, 0)
-            copy_x(0, "V")
-            inter(1, 0)
-            quant_x(0)
             turn(1)
-            copy_x(1, "S")
+            inter(1, 0, "S")
+            copy_x(0, "V")
+            inter(0, 0, "S")
+            quant_x(0)
+            quant_d(1, 0)
             quant_d(0, 0)
-            inter(0, 1)
+            copy_x(1, "S")
             quant_x(1)
             mm_gc(0, 0)
-            mm_gc(0, 1)
-            quant_d(1, 0)
             copy_gc(0, 0)
+            mm_gc(0, 1)
+            inter(0, 1, "S")
+            mm_gc(1, 1)
             copy_gc(0, 1)
-            mm_gr(0, 0)
-            square_gc(0, R, "G")
-            inter(1, 1)
-            mm_gr(1, 0)
+            inter(1, 1, "S")
             quant_d(0, 1)
             mm_gc(1, 0)
-            turn(3)
             quant_d(1, 1)
-            square_gr(1, 0)
+            mm_gr(1, 0)
             square_gc(0, L, "S")
+            copy_gc(1, 0)
+            square_gr(1, 0)
+            mm_gr(0, 0)
+            turn(3)
             turn(2)
             diagonal(0, 0)
             copy_x(3, "S")
-            mm_gc(1, 1)
-            mm_gr(0, 1)
-            copy_gc(1, 0)
             copy_x(2, "S")
+            mm_gr(0, 1)
+            diagonal(1, 0)
+            mm_gr(1, 1)
+            quant_x(2, 2)
+            square_gc(0, R, "G")
             square_gr(0, 0)
             copy_gc(1, 1)
             square_gr(0, 1)
-            mm_gr(1, 1)
-            quant_x(2, 2)
-            square_gc(1, L, "S")
-            diagonal(1, 0)
             add_squares(0, W, "G")
-            square_gc(1, R, "S")
             diagonal(0, 1)
+            square_gc(1, L, "S")
+            square_gc(1, R, "S")
             for m in range(2, TILES - 2, 2):
-                mm_gc(m, 0)
-                mm_gr(m, 1)
-                mm_gc(m, 1)
-                diagonal(m - 1, 1)
                 square_gr(m - 1, 1)
-                root(m - 2, W)
+                mm_gc(m, 0)
+                mm_gc(m, 1)
+                mm_gr(m, 1)
                 copy_gc(m, 0)
+                square_gr(m, 1)
                 mm_gr(m, 0)
-                mm_gc(m + 1, 0)
                 copy_gc(m, 1)
+                turn(m + 2)
+                diagonal(m - 1, 1)
+                root(m - 2, W)
+                turn(m + 3)
                 square_gc(m, W, "S")
                 diagonal(m, 0)
-                diagonal(m, 1)
-                turn(m + 2)
-                turn(m + 3)
                 copy_x(m + 2, "V")
-                square_gr(m, 1)
-                square_gr(m, 0)
                 add_squares(m - 1, W, "G")
-                mm_gr(m + 1, 0)
                 copy_x(m + 3, "V")
-                mm_gc(m + 1, 1)
-                copy_gc(m + 1, 0)
-                square_gr(m + 1, 0)
-                quant_x(m + 2, 2)
-                copy_gc(m + 1, 1)
-                diagonal(m + 1, 0)
+                mm_gr(m + 1, 0)
+                diagonal(m, 1)
+                square_gr(m, 0)
                 add_squares(m, W, "G")
+                square_gr(m + 1, 0)
                 root(m - 1, W)
-                mm_gr(m + 1, 1)
-                square_gc(m + 1, R, "G")
+                quant_x(m + 2, 2)
+                mm_gc(m + 1, 0)
+                copy_gc(m + 1, 0)
                 square_gc(m + 1, L, "S")
-            mm_gc(14, 0)
-            mm_gr(15, 0)
+                mm_gc(m + 1, 1)
+                copy_gc(m + 1, 1)
+                square_gc(m + 1, R, "G")
+                diagonal(m + 1, 0)
+                mm_gr(m + 1, 1)
             square_gr(13, 1)
-            copy_gc(14, 0)
-            mm_gc(15, 1)
             mm_gc(14, 1)
-            add_squares(13, W, "G")
-            mm_gc(15, 0)
-            copy_gc(15, 1)
-            copy_gc(14, 1)
             mm_gr(14, 0)
+            mm_gc(14, 0)
             diagonal(13, 1)
-            root(12, W)
-            square_gc(14, W, "S")
             mm_gr(14, 1)
+            mm_gc(15, 0)
+            copy_gc(14, 1)
             square_gr(14, 0)
-            copy_gc(15, 0)
+            copy_gc(14, 0)
+            root(12, W)
             square_gr(14, 1)
-            diagonal(15, 0)
-            square_gc(15, L, "V")
             diagonal(14, 0)
+            square_gc(14, W, "S")
+            copy_gc(15, 0)
+            mm_gr(15, 0)
+            mm_gc(15, 1)
             square_gr(15, 0)
             diagonal(14, 1)
-            add_squares(15, L, "V")
-            root(13, W)
-            add_squares(14, L, "G")
             mm_gr(15, 1)
-            add_squares(14, R, "G")
-            root(15, L)
+            copy_gc(15, 1)
+            add_squares(13, W, "G")
             diagonal(15, 1)
+            add_squares(14, L, "V")
+            square_gc(15, L, "S")
+            root(13, W)
+            add_squares(14, R, "G")
             square_gc(15, R, "V")
             square_gr(15, 1)
-            root(14, W)
+            add_squares(15, L, "V")
             add_squares(15, R, "V")
+            root(14, W)
+            root(15, L)
+            diagonal(15, 0)
             root(15, R)

@@ -32,7 +32,7 @@ def tile_patch_gradient_magnitude_s1_kernel(tc, patches, d_row, d_col_words, d_c
     with ExitStack() as ctx:
         keep = ctx.enter_context(tc.tile_pool(name="keep", bufs=1))
         stage = ctx.enter_context(tc.tile_pool(name="stage", bufs=3))
-        work = ctx.enter_context(tc.tile_pool(name="work", bufs=4))
+        work = ctx.enter_context(tc.tile_pool(name="work", bufs=5))
         outs = ctx.enter_context(tc.tile_pool(name="outs", bufs=5))
         psum = ctx.enter_context(tc.psum_pool(name="psum", bufs=3))
         psum_t = ctx.enter_context(tc.psum_pool(name="psum_t", bufs=2))
@@ -198,128 +198,128 @@ def tile_patch_gradient_magnitude_s1_kernel(tc, patches, d_row, d_col_words, d_c
         with tc.manual_schedule():
             load_x(0, 1)
             load_d_row(1, 0)
-            load_d_row(0, 0)
             load_scales()
+            load_d_row(0, 0)
             load_x(1, 1)
             load_words(0)
             load_words(1)
             load_d_row(0, 1)
             load_d_row(1, 1)
             load_x(2, 2)
+            load_x(12, 2)
             load_x(4, 2)
-            load_x(6, 2)
+            load_x(14, 2)
             load_x(8, 2)
             load_x(10, 2)
-            load_x(12, 2)
-            load_x(14, 2)
+            load_x(6, 2)
             nc.scalar.activation(out=warm[:], in_=one[:], func=ACT.Sqrt, bias=FLOOR_SQUARED)
             turn(0)
             turn(1)
             inter(1, 0, "S")
             copy_x(0, "V")
             inter(0, 0, "S")
+            copy_x(1, "S")
             quant_x(0)
             quant_d(1, 0)
-            quant_d(0, 0)
-            copy_x(1, "S")
-            quant_x(1)
             mm_gc(0, 0)
-            copy_gc(0, 0)
             mm_gc(0, 1)
+            quant_d(0, 0)
+            quant_x(1)
+            copy_gc(0, 0)
             inter(0, 1, "S")
-            mm_gc(1, 1)
             copy_gc(0, 1)
+            mm_gc(1, 0)
             inter(1, 1, "S")
             quant_d(0, 1)
-            mm_gc(1, 0)
-            quant_d(1, 1)
             mm_gr(1, 0)
-            square_gc(0, L, "S")
-            copy_gc(1, 0)
-            square_gr(1, 0)
             mm_gr(0, 0)
             turn(3)
+            square_gr(1, 0)
             turn(2)
-            diagonal(0, 0)
+            quant_d(1, 1)
+            mm_gr(0, 1)
+            square_gc(0, L, "S")
             copy_x(3, "S")
             copy_x(2, "S")
-            mm_gr(0, 1)
-            diagonal(1, 0)
-            mm_gr(1, 1)
-            quant_x(2, 2)
-            square_gc(0, R, "G")
-            square_gr(0, 0)
-            copy_gc(1, 1)
             square_gr(0, 1)
-            add_squares(0, W, "G")
-            diagonal(0, 1)
+            copy_gc(1, 0)
+            mm_gc(1, 1)
+            square_gc(0, R, "G")
+            diagonal(0, 0)
+            square_gr(0, 0)
+            diagonal(1, 0)
             square_gc(1, L, "S")
+            quant_x(2, 2)
+            copy_gc(1, 1)
+            add_squares(0, W, "G")
+            mm_gr(1, 1)
+            diagonal(0, 1)
             square_gc(1, R, "S")
             for m in range(2, TILES - 2, 2):
                 square_gr(m - 1, 1)
-                mm_gc(m, 0)
                 mm_gc(m, 1)
+                mm_gc(m, 0)
                 mm_gr(m, 1)
-                copy_gc(m, 0)
+                copy_gc(m, 1)
                 square_gr(m, 1)
                 mm_gr(m, 0)
-                copy_gc(m, 1)
                 turn(m + 2)
-                diagonal(m - 1, 1)
-                root(m - 2, W)
+                copy_gc(m, 0)
                 turn(m + 3)
-                square_gc(m, W, "S")
+                diagonal(m - 1, 1)
                 diagonal(m, 0)
                 copy_x(m + 2, "V")
-                add_squares(m - 1, W, "G")
-                copy_x(m + 3, "V")
                 mm_gr(m + 1, 0)
+                root(m - 2, W)
+                square_gc(m, W, "S")
+                mm_gc(m + 1, 0)
+                copy_x(m + 3, "V")
                 diagonal(m, 1)
+                mm_gc(m + 1, 1)
+                quant_x(m + 2, 2)
                 square_gr(m, 0)
-                add_squares(m, W, "G")
+                copy_gc(m + 1, 0)
+                add_squares(m - 1, W, "G")
+                copy_gc(m + 1, 1)
                 square_gr(m + 1, 0)
                 root(m - 1, W)
-                quant_x(m + 2, 2)
-                mm_gc(m + 1, 0)
-                copy_gc(m + 1, 0)
-                square_gc(m + 1, L, "S")
-                mm_gc(m + 1, 1)
-                copy_gc(m + 1, 1)
-                square_gc(m + 1, R, "G")
                 diagonal(m + 1, 0)
+                add_squares(m, W, "G")
+                square_gc(m + 1, R, "G")
+                square_gc(m + 1, L, "S")
                 mm_gr(m + 1, 1)
-            square_gr(13, 1)
-            mm_gc(14, 1)
             mm_gr(14, 0)
+            square_gr(13, 1)
             mm_gc(14, 0)
-            diagonal(13, 1)
-            mm_gr(14, 1)
-            mm_gc(15, 0)
-            copy_gc(14, 1)
-            square_gr(14, 0)
+            mm_gc(14, 1)
             copy_gc(14, 0)
-            root(12, W)
-            square_gr(14, 1)
-            diagonal(14, 0)
-            square_gc(14, W, "S")
-            copy_gc(15, 0)
-            mm_gr(15, 0)
-            mm_gc(15, 1)
-            square_gr(15, 0)
-            diagonal(14, 1)
-            mm_gr(15, 1)
-            copy_gc(15, 1)
+            diagonal(13, 1)
             add_squares(13, W, "G")
+            square_gr(14, 0)
+            mm_gr(14, 1)
+            copy_gc(14, 1)
+            root(12, W)
+            mm_gc(15, 0)
+            mm_gc(15, 1)
+            diagonal(14, 0)
+            square_gr(14, 1)
+            copy_gc(15, 0)
+            mm_gr(15, 1)
+            mm_gr(15, 0)
+            square_gc(14, W, "S")
+            copy_gc(15, 1)
+            diagonal(14, 1)
+            square_gc(15, L, "S")
+            square_gr(15, 0)
             diagonal(15, 1)
             add_squares(14, L, "V")
-            square_gc(15, L, "S")
+            add_squares(14, R, "V")
             root(13, W)
-            add_squares(14, R, "G")
-            square_gc(15, R, "V")
             square_gr(15, 1)
             add_squares(15, L, "V")
-            add_squares(15, R, "V")
+            square_gc(15, R, "V")
             root(14, W)
-            root(15, L)
+            add_squares(15, R, "V")
             diagonal(15, 0)
+            root(15, L)
             root(15, R)

from contextlib import ExitStack

import concourse.mybir as mybir
from concourse.masks import make_identity

F32 = mybir.dt.float32
BF16 = mybir.dt.bfloat16
U32 = mybir.dt.uint32
I32 = mybir.dt.int32
U8 = mybir.dt.uint8
FP8X4 = mybir.dt.float8_e4m3fn_x4
FP4X4 = mybir.dt.float4_e2m1fn_x4
ACT = mybir.ActivationFunctionType
ALU = mybir.AluOpType

M, K, N = 2048, 1024, 1024
P = 128
PACK = 4
K_PASS = P * PACK
PASSES = K // K_PASS
HALF = 512
TILES = M // P
FLOOR_SQUARED = 0.0625
FLOPS = 2 * 2 * M * K * N
S_COLS = 256
GCB, GRB = 3, 3
L, R, W = slice(0, HALF), slice(HALF, N), slice(0, N)


def tile_patch_gradient_magnitude_s1_kernel(tc, patches, d_row, d_col_words, d_col_scales, out_0, out_1):
    nc = tc.nc
    with ExitStack() as ctx:
        keep = ctx.enter_context(tc.tile_pool(name="keep", bufs=1))
        stage = ctx.enter_context(tc.tile_pool(name="stage", bufs=3))
        work = ctx.enter_context(tc.tile_pool(name="work", bufs=5))
        outs = ctx.enter_context(tc.tile_pool(name="outs", bufs=5))
        psum = ctx.enter_context(tc.psum_pool(name="psum", bufs=3))
        psum_t = ctx.enter_context(tc.psum_pool(name="psum_t", bufs=2))

        ident = keep.tile([P, P], F32)
        one = keep.tile([P, 1], F32)
        warm = keep.tile([P, 1], F32)
        x_raw = keep.tile([P, TILES, K], BF16, align_bytes=64)
        dr_raw = keep.tile([P, PASSES, 2, PACK, HALF], BF16, align_bytes=64)
        dr_grouped = keep.tile([P, PASSES, 2, HALF, PACK], BF16, align_bytes=64)
        dr_codes = keep.tile([P, PASSES, N], U32, align_bytes=64)
        dr_scales = keep.tile([P, PASSES, N], U8, align_bytes=64)
        dc_words = keep.tile([P, PASSES, 2 * N], U8, align_bytes=64)
        dc_scales = keep.tile([P, PASSES, N], U8, align_bytes=64)

        x_codes, x_scales, x_turned, x_grouped = {}, {}, {}, {}
        gc_bank, gr_bank, gc_sb, gc_sq, gr_sq, total, diag, mag = {}, {}, {}, {}, {}, {}, {}, {}
        engines = {"S": nc.scalar, "V": nc.vector, "G": nc.gpsimd}

        def pair_rows(tensor, m):
            first = m // 2 * 2 * P
            return tensor[first : first + 2 * P, :].rearrange("(p a) k -> p a k", a=2)

        def load_x(m, count):
            nc.sync.dma_start(out=x_raw[:, m : m + count, :], in_=pair_rows(patches, m)[:, m % 2 : m % 2 + count, :])

        def load_d_row(g, h):
            rows = d_row[g * K_PASS : (g + 1) * K_PASS, h * HALF : (h + 1) * HALF]
            nc.sync.dma_start(out=dr_raw[:, g, h, :, :], in_=rows.rearrange("(p j) w -> p j w", j=PACK))

        def load_words(g):
            nc.sync.dma_start(out=dc_words[:, g, :].bitcast(I32), in_=d_col_words[g].bitcast(I32))

        def load_scales():
            for q in range(4):
                nc.sync.dma_start(
                    out=dc_scales[32 * q : 32 * q + 4, :, :].bitcast(I32),
                    in_=d_col_scales[:, 4 * q : 4 * q + 4, :].rearrange("g r n -> r g n").bitcast(I32),
                )

        def turn(m):
            xt = psum_t.tile([P, PASSES, 2, P], F32)
            words = x_raw[:, m, :].bitcast(F32)
            for g in range(PASSES):
                for u in range(2):
                    nc.tensor.transpose(xt[:, g, u, :], words[:, 256 * g + u : 256 * (g + 1) : 2], ident[:])
            x_turned[m] = xt

        def copy_x(m, e):
            if m // 2 not in x_grouped:
                grouped = stage.tile([P, 2, PASSES, P, PACK], BF16, align_bytes=64)
                codes = stage.tile([P, 2, PASSES * P], U32, align_bytes=64)
                scales = stage.tile([P, 2, PASSES * P], U8, align_bytes=64)
                x_grouped[m // 2], x_codes[m // 2], x_scales[m // 2] = grouped, codes, scales
            dst = x_grouped[m // 2][:, m % 2, :, :, :].bitcast(F32)
            src = x_turned[m][:].rearrange("p g u r -> p g r u")
            if e == "S":
                nc.scalar.copy(out=dst, in_=src)
            else:
                nc.vector.tensor_copy(out=dst, in_=src)

        def quant_x(m, count=1):
            pair, a, b = m // 2, m % 2, m % 2 + count
            nc.vector.quantize_mx(
                out=x_codes[pair][:, a:b, :].rearrange("p a w -> p (a w)").bitcast(FP8X4),
                scales=x_scales[pair][:, a:b, :].rearrange("p a w -> p (a w)"),
                in_=x_grouped[pair][:, a:b, :, :, :].rearrange("p a g r t -> p (a g r t)"),
            )

        def inter(g, h, e="S"):
            dst = dr_grouped[:, g, h, :, :].rearrange("p (c i) t -> p c t i", i=4)
            src = dr_raw[:, g, h, :, :].rearrange("p t (c i) -> p c t i", i=4)
            cut = S_COLS // 4
            if e == "S":
                nc.scalar.copy(out=dst[:, :cut], in_=src[:, :cut])
            else:
                nc.gpsimd.tensor_scalar(out=dst[:, :cut], in0=src[:, :cut], scalar1=1.0, scalar2=0.0, op0=ALU.mult, op1=ALU.add)
            nc.vector.tensor_copy(out=dst[:, cut:], in_=src[:, cut:])

        def quant_d(g, h):
            cols = slice(h * HALF, (h + 1) * HALF)
            nc.vector.quantize_mx(
                out=dr_codes[:, g, cols].bitcast(FP8X4),
                scales=dr_scales[:, g, cols],
                in_=dr_grouped[:, g, h, :, :].rearrange("p n t -> p (n t)"),
            )

        def product(acc, m, words, scales):
            for g in range(PASSES):
                rows = slice(g * P, (g + 1) * P)
                nc.tensor.matmul_mx(
                    out=acc[:],
                    lhsT=x_codes[m // 2][:, m % 2, rows].bitcast(FP8X4),
                    lhsT_scale=x_scales[m // 2][:, m % 2, rows],
                    rhs=words(g),
                    rhs_scale=scales[g],
                    start=(g == 0),
                    stop=(g == PASSES - 1),
                )

        def mm_gc(m, h):
            acc_c = psum.tile([P, HALF], F32, bufs=GCB)
            cols = slice(h * HALF, (h + 1) * HALF)
            product(acc_c, m, lambda g: dc_words[:, g, 2 * h * HALF : 2 * (h + 1) * HALF].bitcast(FP4X4), [dc_scales[:, g, cols] for g in range(PASSES)])
            gc_bank[m, h] = acc_c

        def mm_gr(m, h):
            acc_r = psum.tile([P, HALF], F32, bufs=GRB)
            cols = slice(h * HALF, (h + 1) * HALF)
            product(acc_r, m, lambda g: dr_codes[:, g, cols].bitcast(FP8X4), [dr_scales[:, g, cols] for g in range(PASSES)])
            gr_bank[m, h] = acc_r

        def copy_gc(m, h):
            if m not in gc_sb:
                gc = work.tile([P, N], F32)
                gc_sb[m] = gc
            nc.vector.tensor_copy(out=gc_sb[m][:, h * HALF : (h + 1) * HALF], in_=gc_bank[m, h][:])

        def square_gc(m, cols, e="S"):
            if m not in gc_sq:
                gc2 = work.tile([P, N], F32)
                gc_sq[m] = gc2
            gc = gc_sb[m][:, cols]
            if e == "S":
                nc.scalar.activation(out=gc_sq[m][:, cols], in_=gc, func=ACT.Square)
            else:
                engines[e].tensor_tensor(out=gc_sq[m][:, cols], in0=gc, in1=gc, op=ALU.mult)

        def diagonal(m, h):
            if m not in diag:
                dg = outs.tile([P, N], F32)
                diag[m] = dg
            cols = slice(h * HALF, (h + 1) * HALF)
            nc.vector.tensor_tensor(out=diag[m][:, cols], in0=gr_bank[m, h][:], in1=gc_sb[m][:, cols], op=ALU.add)
            if m == TILES - 1:
                nc.sync.dma_start(out=pair_rows(out_1, m)[:, m % 2, cols], in_=diag[m][:, cols])
            elif h == 1:
                nc.sync.dma_start(out=pair_rows(out_1, m)[:, m % 2, :], in_=diag[m][:])

        def square_gr(m, h):
            if m not in gr_sq:
                gr2 = work.tile([P, N], F32)
                gr_sq[m] = gr2
            nc.scalar.activation(out=gr_sq[m][:, h * HALF : (h + 1) * HALF], in_=gr_bank[m, h][:], func=ACT.Square)

        def add_squares(m, cols, e="G"):
            if m not in total:
                sm = work.tile([P, N], F32)
                total[m] = sm
            engines[e].tensor_tensor(out=total[m][:, cols], in0=gr_sq[m][:, cols], in1=gc_sq[m][:, cols], op=ALU.add)

        def root(m, cols):
            if m not in mag:
                mg = outs.tile([P, N], F32)
                mag[m] = mg
            nc.scalar.activation(out=mag[m][:, cols], in_=total[m][:, cols], func=ACT.Sqrt, bias=FLOOR_SQUARED)
            nc.sync.dma_start(out=pair_rows(out_0, m)[:, m % 2, cols], in_=mag[m][:, cols])

        nc.vector.memset(dc_scales[:].rearrange("p g n -> p (g n)").bitcast(I32), 0)
        nc.gpsimd.memset(one[:], 1.0)
        make_identity(nc, ident[:])

        with tc.manual_schedule():
            load_x(0, 1)
            load_d_row(1, 0)
            load_scales()
            load_d_row(0, 0)
            load_x(1, 1)
            load_words(0)
            load_words(1)
            load_d_row(0, 1)
            load_d_row(1, 1)
            load_x(2, 2)
            load_x(12, 2)
            load_x(4, 2)
            load_x(14, 2)
            load_x(8, 2)
            load_x(10, 2)
            load_x(6, 2)
            nc.scalar.activation(out=warm[:], in_=one[:], func=ACT.Sqrt, bias=FLOOR_SQUARED)
            turn(0)
            turn(1)
            inter(1, 0, "S")
            copy_x(0, "V")
            inter(0, 0, "S")
            copy_x(1, "S")
            quant_x(0)
            quant_d(1, 0)
            mm_gc(0, 0)
            mm_gc(0, 1)
            quant_d(0, 0)
            quant_x(1)
            copy_gc(0, 0)
            inter(0, 1, "S")
            copy_gc(0, 1)
            mm_gc(1, 0)
            inter(1, 1, "S")
            quant_d(0, 1)
            mm_gr(1, 0)
            mm_gr(0, 0)
            turn(3)
            square_gr(1, 0)
            turn(2)
            quant_d(1, 1)
            mm_gr(0, 1)
            square_gc(0, L, "S")
            copy_x(3, "S")
            copy_x(2, "S")
            square_gr(0, 1)
            copy_gc(1, 0)
            mm_gc(1, 1)
            square_gc(0, R, "G")
            diagonal(0, 0)
            square_gr(0, 0)
            diagonal(1, 0)
            square_gc(1, L, "S")
            quant_x(2, 2)
            copy_gc(1, 1)
            add_squares(0, W, "G")
            mm_gr(1, 1)
            diagonal(0, 1)
            square_gc(1, R, "S")
            for m in range(2, TILES - 2, 2):
                square_gr(m - 1, 1)
                mm_gc(m, 1)
                mm_gc(m, 0)
                mm_gr(m, 1)
                copy_gc(m, 1)
                square_gr(m, 1)
                mm_gr(m, 0)
                turn(m + 2)
                copy_gc(m, 0)
                turn(m + 3)
                diagonal(m - 1, 1)
                diagonal(m, 0)
                copy_x(m + 2, "V")
                mm_gr(m + 1, 0)
                root(m - 2, W)
                square_gc(m, W, "S")
                mm_gc(m + 1, 0)
                copy_x(m + 3, "V")
                diagonal(m, 1)
                mm_gc(m + 1, 1)
                quant_x(m + 2, 2)
                square_gr(m, 0)
                copy_gc(m + 1, 0)
                add_squares(m - 1, W, "G")
                copy_gc(m + 1, 1)
                square_gr(m + 1, 0)
                root(m - 1, W)
                diagonal(m + 1, 0)
                add_squares(m, W, "G")
                square_gc(m + 1, R, "G")
                square_gc(m + 1, L, "S")
                mm_gr(m + 1, 1)
            mm_gr(14, 0)
            square_gr(13, 1)
            mm_gc(14, 0)
            mm_gc(14, 1)
            copy_gc(14, 0)
            diagonal(13, 1)
            add_squares(13, W, "G")
            square_gr(14, 0)
            mm_gr(14, 1)
            copy_gc(14, 1)
            root(12, W)
            mm_gc(15, 0)
            mm_gc(15, 1)
            diagonal(14, 0)
            square_gr(14, 1)
            copy_gc(15, 0)
            mm_gr(15, 1)
            mm_gr(15, 0)
            square_gc(14, W, "S")
            copy_gc(15, 1)
            diagonal(14, 1)
            square_gc(15, L, "S")
            square_gr(15, 0)
            diagonal(15, 1)
            add_squares(14, L, "V")
            add_squares(14, R, "V")
            root(13, W)
            square_gr(15, 1)
            add_squares(15, L, "V")
            square_gc(15, R, "V")
            root(14, W)
            add_squares(15, R, "V")
            diagonal(15, 0)
            root(15, L)
            root(15, R)
